import numpy as np
import ml_dtypes


def mxq(x, axis, fmt="e4m3"):
    dtype, down = {"e4m3": (ml_dtypes.float8_e4m3fn, 7), "e5m2": (ml_dtypes.float8_e5m2, 14)}[fmt]
    v = np.moveaxis(np.asarray(x, np.float32).astype(ml_dtypes.bfloat16).astype(np.float64), axis, -1)
    blocks = v.reshape(v.shape[:-1] + (-1, 32))
    amax = np.abs(blocks).max(-1, keepdims=True)
    byte = np.maximum(np.where(amax > 0, np.frexp(amax)[1] - 1 + 127, 0) - down, 1)
    scale = np.exp2(byte - 127.0)
    codes = (blocks / scale).astype(np.float32).astype(dtype).astype(np.float64)
    return np.moveaxis((codes * scale).reshape(v.shape), -1, axis)


WIDE = False


def mx_kscale(k):
    if not WIDE:
        return np.ones(k)
    levels = np.array([30, -30])
    if k % 512:
        return np.exp2(np.random.permutation(np.resize(levels, k // 32))).repeat(32)
    a = np.empty((k // 512, 16))
    for p in range(k // 512):
        a[p, :8] = np.random.permutation(np.resize(levels, 8))
        for g in range(8):
            far = levels[np.abs(levels - a[p, g]) >= 10]
            a[p, g + 8] = far[np.random.randint(len(far))]
    return np.exp2(a.ravel()).repeat(32)


def f64(x):
    return np.asarray(x).astype(np.float64)


def striped(idx):
    return np.tile(np.asarray(idx).reshape(-1, 16).T, (8, 1)).astype(np.uint16)


def unstriped(offs):
    return offs[:16].T.reshape(-1).astype(np.int64)


E2M1 = np.array([0.0, 0.5, 1.0, 1.5, 2.0, 3.0, 4.0, 6.0, -0.0, -0.5, -1.0, -1.5, -2.0, -3.0, -4.0, -6.0])


def pack_weight(w, fmt):
    k, n = w.shape
    w = f64(np.asarray(w, np.float32).astype(ml_dtypes.bfloat16)).reshape(k // 32, 32, n)
    amax = np.abs(w).max(1)
    if fmt in ("e4m3", "e5m2"):
        byte = np.frexp(amax)[1] - 1 + 127 - (7 if fmt == "e4m3" else 14)
    else:
        mant, ex = np.frexp(amax / 6.0)
        byte = np.where(mant > 0.5, ex, ex - 1) + 127
    byte = np.clip(np.where(amax > 0, byte, 1), 1, 254)
    scaled = (w * np.exp2(127.0 - byte)[:, None, :]).reshape(k, n).astype(np.float32)
    by_word = np.ascontiguousarray(scaled.reshape(k // 512, 128, 4, n).transpose(0, 1, 3, 2))
    if fmt in ("e4m3", "e5m2"):
        words = by_word.astype(ml_dtypes.float8_e4m3fn if fmt == "e4m3" else ml_dtypes.float8_e5m2).view(np.uint8)
    else:
        c = by_word.astype(ml_dtypes.float4_e2m1fn).view(np.uint8) & 0xF
        words = (c[..., 0::2] | (c[..., 1::2] << 4)).reshape(k // 512, 128, 2 * n)
    return np.ascontiguousarray(words), np.ascontiguousarray(byte.astype(np.uint8).reshape(k // 512, 16, n))


def unpack_weight(words, scales, fmt):
    g, _, n = scales.shape
    words = np.ascontiguousarray(words).reshape(g, 128, n, -1)
    if fmt in ("e4m3", "e5m2"):
        vals = words.view(ml_dtypes.float8_e4m3fn if fmt == "e4m3" else ml_dtypes.float8_e5m2).astype(np.float64)
    else:
        nib = np.empty((g, 128, n, 4), np.uint8)
        nib[..., 0::2] = words & 0xF
        nib[..., 1::2] = words >> 4
        vals = E2M1[nib]
    vals = vals * np.repeat(np.exp2(scales.astype(np.float64) - 127.0), 8, axis=1)[..., None]
    return vals.transpose(0, 1, 3, 2).reshape(g * 512, n)


K, T, I, J, N, Z, S, V, C, O = 512, 1024, 512, 256, 256, 1024, 1024, 1024, 512, 256


def setup_inputs():
    n = np.random.standard_normal
    idx = np.random.permutation(T)[:I]
    idx2 = np.random.permutation(Z)[:J]
    idx3 = np.random.permutation(V)[:J]
    idx4 = np.random.permutation(C)[:J]
    idx5 = np.random.permutation(C)[:J]
    idx6 = np.random.permutation(C)[:O]
    idx7 = np.random.permutation(S)[:N]
    fk = mx_kscale(K)
    fi = mx_kscale(I)
    ti = np.ones(T)
    ti[idx] = fi
    xkp = pack_weight(n((K, T)) * 0.3 * fk[:, None] * ti, "e5m2")
    xqp = pack_weight(n((K, Z)) * 0.3 / fk[:, None], "e2m1")
    xrp = pack_weight(n((K, V)) * 0.3 / fk[:, None], "e5m2")
    vsp = pack_weight(n((I, S)) / fi[:, None], "e5m2")
    return {
        "xk_words": xkp[0],
        "xk_scales": xkp[1],
        "xq_words": xqp[0],
        "xq_scales": xqp[1],
        "xr_words": xrp[0],
        "xr_scales": xrp[1],
        "vs_words": vsp[0],
        "vs_scales": vsp[1],
        "offs": striped(idx),
        "offs2": striped(idx2),
        "offs3": striped(idx3),
        "offs4": striped(idx4),
        "offs5": striped(idx5),
        "offs6": striped(idx6),
        "offs7": striped(idx7),
    }


def reference(xk_words, xk_scales, xq_words, xq_scales, xr_words, xr_scales, vs_words, vs_scales, offs, offs2, offs3, offs4, offs5, offs6, offs7):
    idx = unstriped(offs)
    idx2 = unstriped(offs2)
    idx3 = unstriped(offs3)
    idx4 = unstriped(offs4)
    idx5 = unstriped(offs5)
    idx6 = unstriped(offs6)
    idx7 = unstriped(offs7)
    xku = unpack_weight(xk_words, xk_scales, "e5m2")
    xqu = unpack_weight(xq_words, xq_scales, "e2m1")
    xru = unpack_weight(xr_words, xr_scales, "e5m2")
    vsu = unpack_weight(vs_words, vs_scales, "e5m2")
    xkidxg = xku[:, idx]
    xqidx2g = xqu[:, idx2]
    s1 = xkidxg.T @ xqidx2g
    xridx3g = xru[:, idx3]
    s2 = xkidxg.T @ xridx3g
    pw = np.zeros((I, C))
    pw[:, idx4] = s1
    pv = np.zeros((I, C))
    pv[:, idx5] = s2
    pg = pw + pv
    hid = pg[:, idx6]
    vsidx7g = vsu[:, idx7]
    hidq = mxq(hid, 0, "e4m3")
    y = vsidx7g.T @ hidq
    return y

@@ -1,0 +1,196 @@
+from contextlib import ExitStack
+
+import concourse.mybir as mybir
+
+FLOPS = 335544320
+
+F32 = mybir.dt.float32
+BF16 = mybir.dt.bfloat16
+I32 = mybir.dt.int32
+U32 = mybir.dt.uint32
+U16 = mybir.dt.uint16
+U8 = mybir.dt.uint8
+E4M3 = mybir.dt.float8_e4m3fn_x4
+E5M2 = mybir.dt.float8_e5m2_x4
+E2M1 = mybir.dt.float4_e2m1fn_x4
+COPY = mybir.ActivationFunctionType.Copy
+ADD = mybir.AluOpType.add
+
+P = 128
+PACK = 4
+TABLE = 1024
+ROWS = 512
+COLS = 256
+BOARD = 512
+HALF = 128
+LIST_HALF = HALF // 16
+
+
+def tile_list_contest_rivals_shared_plain_kernel(
+    tc, xk_words, xk_scales, xq_words, xq_scales, xr_words, xr_scales, vs_words, vs_scales,
+    offs, offs2, offs3, offs4, offs5, offs6, offs7, out,
+):
+    nc = tc.nc
+    with ExitStack() as ctx:
+        keep = ctx.enter_context(tc.tile_pool(name="keep", bufs=1))
+        psum = ctx.enter_context(tc.psum_pool(name="psum", bufs=8))
+
+        def sbuf(name, shape, dtype):
+            return keep.tile(shape, dtype, name=name, align_bytes=64)
+
+        def load_list(name, src):
+            entries = sbuf(name, list(src.shape), U16)
+            nc.sync.dma_start(entries[:], src)
+            return entries
+
+        def load_words(name, src, dtype):
+            words = sbuf(name, [P, TABLE], dtype)
+            nc.sync.dma_start(words[:].bitcast(I32), src.bitcast(I32))
+            return words
+
+        def load_plane(plane, src, queue, quadrants):
+            for q in quadrants:
+                rows = src[0, 4 * q : 4 * q + 4, :].bitcast(I32)
+                queue.dma_start(plane[32 * q : 32 * q + 32, :].bitcast(I32), rows.partition_broadcast(8))
+
+        def gather(name, table, entries, dtype):
+            picked = sbuf(name, [P, COLS], dtype)
+            nc.vector.tensor_copy(picked[:], table[:].indirect(entries[:]))
+            return picked
+
+        def gather_dealt(name, table, entries, dtype):
+            picked = sbuf(name, [P, ROWS], dtype)
+            nc.vector.tensor_copy(picked[:].rearrange("p (t m) -> p m t", t=PACK), table[:].indirect(entries[:]))
+            return picked
+
+        merged = "p n t -> p (n t)"
+
+        xk_plane = sbuf("xk_plane", [P, TABLE], U8)
+        xq_plane = sbuf("xq_plane", [P, TABLE], U8)
+        xr_plane = sbuf("xr_plane", [P, TABLE], U8)
+        vs_plane = sbuf("vs_plane", [P, TABLE], U8)
+        load_plane(xk_plane, xk_scales, nc.scalar, range(4))
+        key_list = load_list("key_list", offs)
+        query_list = load_list("query_list", offs2)
+        xq_table = load_words("xq_table", xq_words[0], U16)
+        xk_table = load_words("xk_table", xk_words[0].rearrange(merged), U32)
+        load_plane(xq_plane, xq_scales, nc.scalar, range(4))
+        rival_list = load_list("rival_list", offs3)
+        query_places = load_list("query_places", offs4)
+        load_plane(xr_plane, xr_scales, nc.sync, range(1))
+        xr_table = load_words("xr_table", xr_words[0].rearrange(merged), U32)
+        load_plane(xr_plane, xr_scales, nc.sync, range(1, 4))
+        rival_places = load_list("rival_places", offs5)
+        store_list = load_list("store_list", offs7)
+        vs_table = load_words("vs_table", vs_words[0].rearrange(merged), U32)
+        load_plane(vs_plane, vs_scales, nc.sync, range(4))
+        read_list = load_list("read_list", offs6)
+
+        pw = [sbuf(f"pw{b}", [P, BOARD], F32) for b in range(2)]
+        pv = [sbuf(f"pv{b}", [P, BOARD], F32) for b in range(3)]
+        for page in pw + pv:
+            nc.vector.memset(page[:], 0.0)
+
+        k_scales = gather_dealt("k_scales", xk_plane, key_list, U8)
+        q_words = gather("q_words", xq_table, query_list, U16)
+        k_words = gather_dealt("k_words", xk_table, key_list, U32)
+        q_scales = gather("q_scales", xq_plane, query_list, U8)
+
+        def scores(name, slices, words, scales):
+            bank = psum.tile([P, len(slices), COLS], F32, name=name, tag="bank")
+            for u, t in enumerate(slices):
+                cols = slice(t * P, (t + 1) * P)
+                nc.tensor.matmul_mx(
+                    out=bank[:, u, :], lhsT=k_words[:, cols].bitcast(E5M2), lhsT_scale=k_scales[:, cols],
+                    rhs=words, rhs_scale=scales[:], start=True, stop=True,
+                )
+            return bank
+
+        groups1 = [(0,), (1,), (2, 3)]
+        groups2 = [(0, 1), (2, 3)]
+        s1_banks = [scores(f"s1_bank{u}", g, q_words[:].bitcast(E2M1), q_scales) for u, g in enumerate(groups1)]
+        r_words = gather("r_words", xr_table, rival_list, U32)
+        r_scales = gather("r_scales", xr_plane, rival_list, U8)
+        s2_banks = [scores(f"s2_bank{u}", g, r_words[:].bitcast(E5M2), r_scales) for u, g in enumerate(groups2)]
+
+        s1_held = [sbuf(f"s1_{u}", [P, len(g), COLS], F32) for u, g in enumerate(groups1)]
+        s2_held = [sbuf(f"s2_{u}", [P, len(g), COLS], F32) for u, g in enumerate(groups2)]
+        s1 = {t: s1_held[u][:, j, :] for u, g in enumerate(groups1) for j, t in enumerate(g)}
+        s2 = {t: s2_held[u][:, j, :] for u, g in enumerate(groups2) for j, t in enumerate(g)}
+        pg = [sbuf(f"pg{t}", [P, BOARD], F32) for t in range(PACK)]
+        hid = sbuf("hid", [P, PACK, COLS], F32)
+
+        def out_scalar(dst, bank):
+            nc.scalar.copy(dst[:], bank[:])
+
+        def out_vector(dst, bank):
+            nc.vector.tensor_copy(dst[:], bank[:])
+
+        def put_scalar(page, places, values):
+            nc.scalar.activation(page[:].indirect(places[:]), values, COPY)
+
+        def put_vector(page, places, values):
+            nc.vector.tensor_copy(page[:].indirect(places[:]), values)
+
+        def add(t, engine):
+            engine.tensor_tensor(pg[t][:], pw[t % len(pw)][:], pv[t % len(pv)][:], ADD)
+
+        def read_vector(t, a, b):
+            nc.vector.tensor_copy(hid[:, t, 16 * a : 16 * b], pg[t][:].indirect(read_list[:, a:b]))
+
+        def read_scalar(t, a, b):
+            nc.scalar.activation(hid[:, t, 16 * a : 16 * b], pg[t][:].indirect(read_list[:, a:b]), COPY)
+
+        whole = 2 * LIST_HALF
+        out_scalar(s1_held[0], s1_banks[0])
+        out_scalar(s1_held[1], s1_banks[1])
+        put_scalar(pw[0], query_places, s1[0])
+        v_words = gather("v_words", vs_table, store_list, U32)
+        out_vector(s2_held[0], s2_banks[0])
+        v_scales = gather("v_scales", vs_plane, store_list, U8)
+        put_scalar(pw[1], query_places, s1[1])
+        put_vector(pv[0], rival_places, s2[0])
+        put_scalar(pv[1], rival_places, s2[1])
+        out_vector(s2_held[1], s2_banks[1])
+        add(0, nc.vector)
+        out_scalar(s1_held[2], s1_banks[2])
+        put_vector(pv[2], rival_places, s2[2])
+        put_scalar(pw[0], query_places, s1[2])
+        add(1, nc.vector)
+        put_vector(pv[0], rival_places, s2[3])
+        put_scalar(pw[1], query_places, s1[3])
+        add(2, nc.vector)
+        read_scalar(0, 0, whole)
+        add(3, nc.vector)
+        read_scalar(1, 0, whole)
+        read_vector(3, 0, whole)
+        read_scalar(2, 0, whole)
+
+        woven = [sbuf(f"woven{h}", [P, HALF * PACK], BF16) for h in range(2)]
+        h_words = [sbuf(f"h_words{h}", [P, HALF], U32) for h in range(2)]
+        h_scales = [sbuf(f"h_scales{h}", [P, HALF], U8) for h in range(2)]
+
+        def weave_views(h):
+            dst = woven[h][:].rearrange("p (c i t) -> p c t i", i=4, t=PACK)
+            src = hid[:, :, h * HALF : (h + 1) * HALF].rearrange("p t (c i) -> p c t i", i=4)
+            return dst, src
+
+        nc.vector.tensor_copy(*weave_views(0))
+        nc.scalar.copy(*weave_views(1))
+        for h in range(2):
+            nc.vector.quantize_mx(out=h_words[h][:].bitcast(E4M3), scales=h_scales[h][:], in_=woven[h][:])
+        for h in range(2):
+            for g in range(2):
+                bank = psum.tile([P, HALF], F32, name=f"y_bank{h}{g}", tag="bank")
+                rows = slice(g * P, (g + 1) * P)
+                nc.tensor.matmul_mx(
+                    out=bank[:], lhsT=v_words[:, rows].bitcast(E5M2), lhsT_scale=v_scales[:, rows],
+                    rhs=h_words[h][:].bitcast(E4M3), rhs_scale=h_scales[h][:], start=True, stop=True,
+                )
+                y = sbuf(f"y{h}{g}", [P, HALF], F32)
+                if g == 0:
+                    out_vector(y, bank)
+                    nc.sync.dma_start(out[rows, h * HALF : (h + 1) * HALF], y[:])
+                else:
+                    out_scalar(y, bank)
+                    nc.scalar.dma_start(out[rows, h * HALF : (h + 1) * HALF], y[:])

@@ -35,26 +35,26 @@ def tile_list_contest_rivals_shared_plain_kernel(
         keep = ctx.enter_context(tc.tile_pool(name="keep", bufs=1))
         psum = ctx.enter_context(tc.psum_pool(name="psum", bufs=8))
 
-        def sbuf(name, shape, dtype):
-            return keep.tile(shape, dtype, name=name, align_bytes=64)
+        def sbuf(name, shape, dtype, tag=None):
+            return keep.tile(shape, dtype, name=name, tag=tag or name, align_bytes=64)
 
         def load_list(name, src):
             entries = sbuf(name, list(src.shape), U16)
             nc.sync.dma_start(entries[:], src)
             return entries
 
-        def load_words(name, src, dtype):
+        def load_words(name, src, dtype, queue):
             words = sbuf(name, [P, TABLE], dtype)
-            nc.sync.dma_start(words[:].bitcast(I32), src.bitcast(I32))
+            queue.dma_start(words[:].bitcast(I32), src.bitcast(I32))
             return words
 
-        def load_plane(plane, src, queue, quadrants):
-            for q in quadrants:
+        def load_plane(plane, src):
+            for q in range(4):
                 rows = src[0, 4 * q : 4 * q + 4, :].bitcast(I32)
-                queue.dma_start(plane[32 * q : 32 * q + 32, :].bitcast(I32), rows.partition_broadcast(8))
+                nc.sync.dma_start(plane[32 * q : 32 * q + 4, :].bitcast(I32), rows)
 
-        def gather(name, table, entries, dtype):
-            picked = sbuf(name, [P, COLS], dtype)
+        def gather(name, table, entries, dtype, tag=None):
+            picked = sbuf(name, [P, COLS], dtype, tag)
             nc.vector.tensor_copy(picked[:], table[:].indirect(entries[:]))
             return picked
 
@@ -69,55 +69,57 @@ def tile_list_contest_rivals_shared_plain_kernel(
         xq_plane = sbuf("xq_plane", [P, TABLE], U8)
         xr_plane = sbuf("xr_plane", [P, TABLE], U8)
         vs_plane = sbuf("vs_plane", [P, TABLE], U8)
-        load_plane(xk_plane, xk_scales, nc.scalar, range(4))
-        key_list = load_list("key_list", offs)
+        nc.vector.memset(xk_plane[:].bitcast(I32), 0)
+        nc.vector.memset(xq_plane[:].bitcast(I32), 0)
+        nc.gpsimd.memset(xr_plane[:].bitcast(I32), 0)
+        nc.gpsimd.memset(vs_plane[:].bitcast(I32), 0)
+        xq_table = load_words("xq_table", xq_words[0], U16, nc.scalar)
+        xk_table = load_words("xk_table", xk_words[0].rearrange(merged), U32, nc.scalar)
         query_list = load_list("query_list", offs2)
-        xq_table = load_words("xq_table", xq_words[0], U16)
-        xk_table = load_words("xk_table", xk_words[0].rearrange(merged), U32)
-        load_plane(xq_plane, xq_scales, nc.scalar, range(4))
+        key_list = load_list("key_list", offs)
+        load_plane(xk_plane, xk_scales)
+        load_plane(xq_plane, xq_scales)
         rival_list = load_list("rival_list", offs3)
+        xr_table = load_words("xr_table", xr_words[0].rearrange(merged), U32, nc.sync)
         query_places = load_list("query_places", offs4)
-        load_plane(xr_plane, xr_scales, nc.sync, range(1))
-        xr_table = load_words("xr_table", xr_words[0].rearrange(merged), U32)
-        load_plane(xr_plane, xr_scales, nc.sync, range(1, 4))
-        rival_places = load_list("rival_places", offs5)
         store_list = load_list("store_list", offs7)
-        vs_table = load_words("vs_table", vs_words[0].rearrange(merged), U32)
-        load_plane(vs_plane, vs_scales, nc.sync, range(4))
+        load_plane(xr_plane, xr_scales)
+        vs_table = load_words("vs_table", vs_words[0].rearrange(merged), U32, nc.sync)
+        rival_places = load_list("rival_places", offs5)
+        load_plane(vs_plane, vs_scales)
         read_list = load_list("read_list", offs6)
 
-        pw = [sbuf(f"pw{b}", [P, BOARD], F32) for b in range(2)]
-        pv = [sbuf(f"pv{b}", [P, BOARD], F32) for b in range(3)]
-        for page in pw + pv:
-            nc.vector.memset(page[:], 0.0)
+        pw = [sbuf(f"pw{b}", [P, BOARD], F32) for b in range(4)]
+        pv = [sbuf(f"pv{b}", [P, BOARD], F32) for b in range(4)]
+        for page in pw[:2] + pv[:2] + pw[2:] + pv[2:]:
+            nc.gpsimd.memset(page[:], 0.0)
 
-        k_scales = gather_dealt("k_scales", xk_plane, key_list, U8)
         q_words = gather("q_words", xq_table, query_list, U16)
         k_words = gather_dealt("k_words", xk_table, key_list, U32)
+        k_scales = gather_dealt("k_scales", xk_plane, key_list, U8)
         q_scales = gather("q_scales", xq_plane, query_list, U8)
 
-        def scores(name, slices, words, scales):
-            bank = psum.tile([P, len(slices), COLS], F32, name=name, tag="bank")
-            for u, t in enumerate(slices):
+        groups = [[(1, 0)], [(1, 1)], [(2, 0), (2, 1)], [(1, 2), (2, 2)], [(1, 3), (2, 3)]]
+        banks = [psum.tile([P, len(g), COLS], F32, name=f"bank{u}", tag="bank") for u, g in enumerate(groups)]
+        held = [sbuf(f"held{u}", [P, len(g), COLS], F32) for u, g in enumerate(groups)]
+        place = {key: (u, j) for u, g in enumerate(groups) for j, key in enumerate(g)}
+
+        def scores(kind, words, scales):
+            for t in range(PACK):
+                u, j = place[(kind, t)]
                 cols = slice(t * P, (t + 1) * P)
                 nc.tensor.matmul_mx(
-                    out=bank[:, u, :], lhsT=k_words[:, cols].bitcast(E5M2), lhsT_scale=k_scales[:, cols],
+                    out=banks[u][:, j, :], lhsT=k_words[:, cols].bitcast(E5M2), lhsT_scale=k_scales[:, cols],
                     rhs=words, rhs_scale=scales[:], start=True, stop=True,
                 )
-            return bank
 
-        groups1 = [(0,), (1,), (2, 3)]
-        groups2 = [(0, 1), (2, 3)]
-        s1_banks = [scores(f"s1_bank{u}", g, q_words[:].bitcast(E2M1), q_scales) for u, g in enumerate(groups1)]
+        scores(1, q_words[:].bitcast(E2M1), q_scales)
         r_words = gather("r_words", xr_table, rival_list, U32)
         r_scales = gather("r_scales", xr_plane, rival_list, U8)
-        s2_banks = [scores(f"s2_bank{u}", g, r_words[:].bitcast(E5M2), r_scales) for u, g in enumerate(groups2)]
-
-        s1_held = [sbuf(f"s1_{u}", [P, len(g), COLS], F32) for u, g in enumerate(groups1)]
-        s2_held = [sbuf(f"s2_{u}", [P, len(g), COLS], F32) for u, g in enumerate(groups2)]
-        s1 = {t: s1_held[u][:, j, :] for u, g in enumerate(groups1) for j, t in enumerate(g)}
-        s2 = {t: s2_held[u][:, j, :] for u, g in enumerate(groups2) for j, t in enumerate(g)}
-        pg = [sbuf(f"pg{t}", [P, BOARD], F32) for t in range(PACK)]
+        scores(2, r_words[:].bitcast(E5M2), r_scales)
+        s1 = [held[place[(1, t)][0]][:, place[(1, t)][1], :] for t in range(PACK)]
+        s2 = [held[place[(2, t)][0]][:, place[(2, t)][1], :] for t in range(PACK)]
+        pg = [sbuf(f"pg{t}", [P, BOARD], F32, f"pg{t % 2}") for t in range(PACK)]
         hid = sbuf("hid", [P, PACK, COLS], F32)
 
         def out_scalar(dst, bank):
@@ -142,29 +144,30 @@ def tile_list_contest_rivals_shared_plain_kernel(
             nc.scalar.activation(hid[:, t, 16 * a : 16 * b], pg[t][:].indirect(read_list[:, a:b]), COPY)
 
         whole = 2 * LIST_HALF
-        out_scalar(s1_held[0], s1_banks[0])
-        out_scalar(s1_held[1], s1_banks[1])
+        out_scalar(held[0], banks[0])
+        out_scalar(held[1], banks[1])
         put_scalar(pw[0], query_places, s1[0])
         v_words = gather("v_words", vs_table, store_list, U32)
-        out_vector(s2_held[0], s2_banks[0])
-        v_scales = gather("v_scales", vs_plane, store_list, U8)
+        out_vector(held[2], banks[2])
         put_scalar(pw[1], query_places, s1[1])
+        out_vector(held[4], banks[4])
         put_vector(pv[0], rival_places, s2[0])
-        put_scalar(pv[1], rival_places, s2[1])
-        out_vector(s2_held[1], s2_banks[1])
-        add(0, nc.vector)
-        out_scalar(s1_held[2], s1_banks[2])
+        out_scalar(held[3], banks[3])
+        put_vector(pv[1], rival_places, s2[1])
+        put_scalar(pw[2], query_places, s1[2])
+        add(0, nc.gpsimd)
         put_vector(pv[2], rival_places, s2[2])
-        put_scalar(pw[0], query_places, s1[2])
-        add(1, nc.vector)
-        put_vector(pv[0], rival_places, s2[3])
-        put_scalar(pw[1], query_places, s1[3])
-        add(2, nc.vector)
-        read_scalar(0, 0, whole)
+        put_scalar(pw[3], query_places, s1[3])
+        add(1, nc.gpsimd)
+        read_vector(0, 0, whole)
+        v_scales = gather("v_scales", vs_plane, store_list, U8, "pw0")
+        put_scalar(pv[3], rival_places, s2[3])
+        add(2, nc.gpsimd)
+        read_vector(1, 0, whole)
         add(3, nc.vector)
-        read_scalar(1, 0, whole)
-        read_vector(3, 0, whole)
         read_scalar(2, 0, whole)
+        read_vector(3, 0, LIST_HALF)
+        read_scalar(3, LIST_HALF, whole)
 
         woven = [sbuf(f"woven{h}", [P, HALF * PACK], BF16) for h in range(2)]
         h_words = [sbuf(f"h_words{h}", [P, HALF], U32) for h in range(2)]

@@ -43,15 +43,15 @@ def tile_list_contest_rivals_shared_plain_kernel(
             nc.sync.dma_start(entries[:], src)
             return entries
 
-        def load_words(name, src, dtype, queue):
+        def load_words(name, src, dtype):
             words = sbuf(name, [P, TABLE], dtype)
-            queue.dma_start(words[:].bitcast(I32), src.bitcast(I32))
+            nc.sync.dma_start(words[:].bitcast(I32), src.bitcast(I32))
             return words
 
-        def load_plane(plane, src):
-            for q in range(4):
+        def load_plane(plane, src, queue, quadrants):
+            for q in quadrants:
                 rows = src[0, 4 * q : 4 * q + 4, :].bitcast(I32)
-                nc.sync.dma_start(plane[32 * q : 32 * q + 4, :].bitcast(I32), rows)
+                queue.dma_start(plane[32 * q : 32 * q + 32, :].bitcast(I32), rows.partition_broadcast(8))
 
         def gather(name, table, entries, dtype, tag=None):
             picked = sbuf(name, [P, COLS], dtype, tag)
@@ -69,34 +69,31 @@ def tile_list_contest_rivals_shared_plain_kernel(
         xq_plane = sbuf("xq_plane", [P, TABLE], U8)
         xr_plane = sbuf("xr_plane", [P, TABLE], U8)
         vs_plane = sbuf("vs_plane", [P, TABLE], U8)
-        nc.vector.memset(xk_plane[:].bitcast(I32), 0)
-        nc.vector.memset(xq_plane[:].bitcast(I32), 0)
-        nc.gpsimd.memset(xr_plane[:].bitcast(I32), 0)
-        nc.gpsimd.memset(vs_plane[:].bitcast(I32), 0)
-        xq_table = load_words("xq_table", xq_words[0], U16, nc.scalar)
-        xk_table = load_words("xk_table", xk_words[0].rearrange(merged), U32, nc.scalar)
-        query_list = load_list("query_list", offs2)
+        load_plane(xk_plane, xk_scales, nc.scalar, range(4))
         key_list = load_list("key_list", offs)
-        load_plane(xk_plane, xk_scales)
-        load_plane(xq_plane, xq_scales)
+        query_list = load_list("query_list", offs2)
+        xq_table = load_words("xq_table", xq_words[0], U16)
+        xk_table = load_words("xk_table", xk_words[0].rearrange(merged), U32)
+        load_plane(xq_plane, xq_scales, nc.scalar, range(4))
         rival_list = load_list("rival_list", offs3)
-        xr_table = load_words("xr_table", xr_words[0].rearrange(merged), U32, nc.sync)
         query_places = load_list("query_places", offs4)
-        store_list = load_list("store_list", offs7)
-        load_plane(xr_plane, xr_scales)
-        vs_table = load_words("vs_table", vs_words[0].rearrange(merged), U32, nc.sync)
+        load_plane(xr_plane, xr_scales, nc.sync, range(1))
+        xr_table = load_words("xr_table", xr_words[0].rearrange(merged), U32)
+        load_plane(xr_plane, xr_scales, nc.sync, range(1, 4))
         rival_places = load_list("rival_places", offs5)
-        load_plane(vs_plane, vs_scales)
+        store_list = load_list("store_list", offs7)
+        vs_table = load_words("vs_table", vs_words[0].rearrange(merged), U32)
+        load_plane(vs_plane, vs_scales, nc.sync, range(4))
         read_list = load_list("read_list", offs6)
 
-        pw = [sbuf(f"pw{b}", [P, BOARD], F32) for b in range(4)]
-        pv = [sbuf(f"pv{b}", [P, BOARD], F32) for b in range(4)]
-        for page in pw[:2] + pv[:2] + pw[2:] + pv[2:]:
-            nc.gpsimd.memset(page[:], 0.0)
+        pw = [sbuf(f"pw{b}", [P, BOARD], F32) for b in range(3)]
+        pv = [sbuf(f"pv{b}", [P, BOARD], F32) for b in range(2)]
+        for page in pw + pv:
+            nc.vector.memset(page[:], 0.0)
 
+        k_scales = gather_dealt("k_scales", xk_plane, key_list, U8)
         q_words = gather("q_words", xq_table, query_list, U16)
         k_words = gather_dealt("k_words", xk_table, key_list, U32)
-        k_scales = gather_dealt("k_scales", xk_plane, key_list, U8)
         q_scales = gather("q_scales", xq_plane, query_list, U8)
 
         groups = [[(1, 0)], [(1, 1)], [(2, 0), (2, 1)], [(1, 2), (2, 2)], [(1, 3), (2, 3)]]
@@ -119,7 +116,7 @@ def tile_list_contest_rivals_shared_plain_kernel(
         scores(2, r_words[:].bitcast(E5M2), r_scales)
         s1 = [held[place[(1, t)][0]][:, place[(1, t)][1], :] for t in range(PACK)]
         s2 = [held[place[(2, t)][0]][:, place[(2, t)][1], :] for t in range(PACK)]
-        pg = [sbuf(f"pg{t}", [P, BOARD], F32, f"pg{t % 2}") for t in range(PACK)]
+        pg = [sbuf(f"pg{t}", [P, BOARD], F32, f"pg{(0, 1, 2, 1)[t]}") for t in range(PACK)]
         hid = sbuf("hid", [P, PACK, COLS], F32)
 
         def out_scalar(dst, bank):
@@ -156,12 +153,12 @@ def tile_list_contest_rivals_shared_plain_kernel(
         put_vector(pv[1], rival_places, s2[1])
         put_scalar(pw[2], query_places, s1[2])
         add(0, nc.gpsimd)
-        put_vector(pv[2], rival_places, s2[2])
-        put_scalar(pw[3], query_places, s1[3])
+        put_vector(pv[0], rival_places, s2[2])
+        put_scalar(pw[0], query_places, s1[3])
         add(1, nc.gpsimd)
         read_vector(0, 0, whole)
-        v_scales = gather("v_scales", vs_plane, store_list, U8, "pw0")
-        put_scalar(pv[3], rival_places, s2[3])
+        v_scales = gather("v_scales", vs_plane, store_list, U8, "pw1")
+        put_scalar(pv[1], rival_places, s2[3])
         add(2, nc.gpsimd)
         read_vector(1, 0, whole)
         add(3, nc.vector)

from contextlib import ExitStack

import concourse.mybir as mybir

FLOPS = 335544320

F32 = mybir.dt.float32
BF16 = mybir.dt.bfloat16
I32 = mybir.dt.int32
U32 = mybir.dt.uint32
U16 = mybir.dt.uint16
U8 = mybir.dt.uint8
E4M3 = mybir.dt.float8_e4m3fn_x4
E5M2 = mybir.dt.float8_e5m2_x4
E2M1 = mybir.dt.float4_e2m1fn_x4
COPY = mybir.ActivationFunctionType.Copy
ADD = mybir.AluOpType.add

P = 128
PACK = 4
TABLE = 1024
ROWS = 512
COLS = 256
BOARD = 512
HALF = 128
LIST_HALF = HALF // 16


def tile_list_contest_rivals_shared_plain_kernel(
    tc, xk_words, xk_scales, xq_words, xq_scales, xr_words, xr_scales, vs_words, vs_scales,
    offs, offs2, offs3, offs4, offs5, offs6, offs7, out,
):
    nc = tc.nc
    with ExitStack() as ctx:
        keep = ctx.enter_context(tc.tile_pool(name="keep", bufs=1))
        psum = ctx.enter_context(tc.psum_pool(name="psum", bufs=8))

        def sbuf(name, shape, dtype, tag=None):
            return keep.tile(shape, dtype, name=name, tag=tag or name, align_bytes=64)

        def load_list(name, src):
            entries = sbuf(name, list(src.shape), U16)
            nc.sync.dma_start(entries[:], src)
            return entries

        def load_words(name, src, dtype):
            words = sbuf(name, [P, TABLE], dtype)
            nc.sync.dma_start(words[:].bitcast(I32), src.bitcast(I32))
            return words

        def load_plane(plane, src, queue, quadrants):
            for q in quadrants:
                rows = src[0, 4 * q : 4 * q + 4, :].bitcast(I32)
                queue.dma_start(plane[32 * q : 32 * q + 32, :].bitcast(I32), rows.partition_broadcast(8))

        def gather(name, table, entries, dtype, tag=None):
            picked = sbuf(name, [P, COLS], dtype, tag)
            nc.vector.tensor_copy(picked[:], table[:].indirect(entries[:]))
            return picked

        def gather_dealt(name, table, entries, dtype):
            picked = sbuf(name, [P, ROWS], dtype)
            nc.vector.tensor_copy(picked[:].rearrange("p (t m) -> p m t", t=PACK), table[:].indirect(entries[:]))
            return picked

        merged = "p n t -> p (n t)"

        xk_plane = sbuf("xk_plane", [P, TABLE], U8)
        xq_plane = sbuf("xq_plane", [P, TABLE], U8)
        xr_plane = sbuf("xr_plane", [P, TABLE], U8)
        vs_plane = sbuf("vs_plane", [P, TABLE], U8)
        load_plane(xk_plane, xk_scales, nc.scalar, range(4))
        key_list = load_list("key_list", offs)
        query_list = load_list("query_list", offs2)
        xq_table = load_words("xq_table", xq_words[0], U16)
        xk_table = load_words("xk_table", xk_words[0].rearrange(merged), U32)
        load_plane(xq_plane, xq_scales, nc.scalar, range(4))
        rival_list = load_list("rival_list", offs3)
        query_places = load_list("query_places", offs4)
        load_plane(xr_plane, xr_scales, nc.sync, range(1))
        xr_table = load_words("xr_table", xr_words[0].rearrange(merged), U32)
        load_plane(xr_plane, xr_scales, nc.sync, range(1, 4))
        rival_places = load_list("rival_places", offs5)
        store_list = load_list("store_list", offs7)
        vs_table = load_words("vs_table", vs_words[0].rearrange(merged), U32)
        load_plane(vs_plane, vs_scales, nc.sync, range(4))
        read_list = load_list("read_list", offs6)

        pw = [sbuf(f"pw{b}", [P, BOARD], F32) for b in range(3)]
        pv = [sbuf(f"pv{b}", [P, BOARD], F32) for b in range(2)]
        for page in pw + pv:
            nc.vector.memset(page[:], 0.0)

        k_scales = gather_dealt("k_scales", xk_plane, key_list, U8)
        q_words = gather("q_words", xq_table, query_list, U16)
        k_words = gather_dealt("k_words", xk_table, key_list, U32)
        q_scales = gather("q_scales", xq_plane, query_list, U8)

        groups = [[(1, 0)], [(1, 1)], [(2, 0), (2, 1)], [(1, 2), (2, 2)], [(1, 3), (2, 3)]]
        banks = [psum.tile([P, len(g), COLS], F32, name=f"bank{u}", tag="bank") for u, g in enumerate(groups)]
        held = [sbuf(f"held{u}", [P, len(g), COLS], F32) for u, g in enumerate(groups)]
        place = {key: (u, j) for u, g in enumerate(groups) for j, key in enumerate(g)}

        def scores(kind, words, scales):
            for t in range(PACK):
                u, j = place[(kind, t)]
                cols = slice(t * P, (t + 1) * P)
                nc.tensor.matmul_mx(
                    out=banks[u][:, j, :], lhsT=k_words[:, cols].bitcast(E5M2), lhsT_scale=k_scales[:, cols],
                    rhs=words, rhs_scale=scales[:], start=True, stop=True,
                )

        scores(1, q_words[:].bitcast(E2M1), q_scales)
        r_words = gather("r_words", xr_table, rival_list, U32)
        r_scales = gather("r_scales", xr_plane, rival_list, U8)
        scores(2, r_words[:].bitcast(E5M2), r_scales)
        s1 = [held[place[(1, t)][0]][:, place[(1, t)][1], :] for t in range(PACK)]
        s2 = [held[place[(2, t)][0]][:, place[(2, t)][1], :] for t in range(PACK)]
        pg = [sbuf(f"pg{t}", [P, BOARD], F32, f"pg{(0, 1, 2, 1)[t]}") for t in range(PACK)]
        hid = sbuf("hid", [P, PACK, COLS], F32)

        def out_scalar(dst, bank):
            nc.scalar.copy(dst[:], bank[:])

        def out_vector(dst, bank):
            nc.vector.tensor_copy(dst[:], bank[:])

        def put_scalar(page, places, values):
            nc.scalar.activation(page[:].indirect(places[:]), values, COPY)

        def put_vector(page, places, values):
            nc.vector.tensor_copy(page[:].indirect(places[:]), values)

        def add(t, engine):
            engine.tensor_tensor(pg[t][:], pw[t % len(pw)][:], pv[t % len(pv)][:], ADD)

        def read_vector(t, a, b):
            nc.vector.tensor_copy(hid[:, t, 16 * a : 16 * b], pg[t][:].indirect(read_list[:, a:b]))

        def read_scalar(t, a, b):
            nc.scalar.activation(hid[:, t, 16 * a : 16 * b], pg[t][:].indirect(read_list[:, a:b]), COPY)

        whole = 2 * LIST_HALF
        out_scalar(held[0], banks[0])
        out_scalar(held[1], banks[1])
        put_scalar(pw[0], query_places, s1[0])
        v_words = gather("v_words", vs_table, store_list, U32)
        out_vector(held[2], banks[2])
        put_scalar(pw[1], query_places, s1[1])
        out_vector(held[4], banks[4])
        put_vector(pv[0], rival_places, s2[0])
        out_scalar(held[3], banks[3])
        put_vector(pv[1], rival_places, s2[1])
        put_scalar(pw[2], query_places, s1[2])
        add(0, nc.gpsimd)
        put_vector(pv[0], rival_places, s2[2])
        put_scalar(pw[0], query_places, s1[3])
        add(1, nc.gpsimd)
        read_vector(0, 0, whole)
        v_scales = gather("v_scales", vs_plane, store_list, U8, "pw1")
        put_scalar(pv[1], rival_places, s2[3])
        add(2, nc.gpsimd)
        read_vector(1, 0, whole)
        add(3, nc.vector)
        read_scalar(2, 0, whole)
        read_vector(3, 0, LIST_HALF)
        read_scalar(3, LIST_HALF, whole)

        woven = [sbuf(f"woven{h}", [P, HALF * PACK], BF16) for h in range(2)]
        h_words = [sbuf(f"h_words{h}", [P, HALF], U32) for h in range(2)]
        h_scales = [sbuf(f"h_scales{h}", [P, HALF], U8) for h in range(2)]

        def weave_views(h):
            dst = woven[h][:].rearrange("p (c i t) -> p c t i", i=4, t=PACK)
            src = hid[:, :, h * HALF : (h + 1) * HALF].rearrange("p t (c i) -> p c t i", i=4)
            return dst, src

        nc.vector.tensor_copy(*weave_views(0))
        nc.scalar.copy(*weave_views(1))
        for h in range(2):
            nc.vector.quantize_mx(out=h_words[h][:].bitcast(E4M3), scales=h_scales[h][:], in_=woven[h][:])
        for h in range(2):
            for g in range(2):
                bank = psum.tile([P, HALF], F32, name=f"y_bank{h}{g}", tag="bank")
                rows = slice(g * P, (g + 1) * P)
                nc.tensor.matmul_mx(
                    out=bank[:], lhsT=v_words[:, rows].bitcast(E5M2), lhsT_scale=v_scales[:, rows],
                    rhs=h_words[h][:].bitcast(E4M3), rhs_scale=h_scales[h][:], start=True, stop=True,
                )
                y = sbuf(f"y{h}{g}", [P, HALF], F32)
                if g == 0:
                    out_vector(y, bank)
                    nc.sync.dma_start(out[rows, h * HALF : (h + 1) * HALF], y[:])
                else:
                    out_scalar(y, bank)
                    nc.scalar.dma_start(out[rows, h * HALF : (h + 1) * HALF], y[:])
